import numpy as np
CORES = [28,29,30,31,156,157,158,159,284,285,286,287,412,413,414,415]
N = 16
def setup_inputs(rng):
    return {"x": rng.standard_normal((N, 128, 64), dtype=np.float32)}
def reference(x):
    p = 128 // N
    blocks = x.reshape(N, N, p, 64)
    return {"y": np.ascontiguousarray(blocks.transpose(1, 0, 2, 3)).reshape(N, 128, 64)}

@@ -1,0 +1,41 @@
+SCRATCH = {
+    "send": ("dram", [16, 128, 4], "float32"),
+    "land": ("dram", [16, 128, 4], "float32"),
+    "relay": ("dram", [4, 128, 4], "float32"),
+}
+SEMAPHORES = ["loaded", "relayed", "arrived", "stored"]
+
+
+def rank_program(g, core, T, topo):
+    r = T.rank_of(core)
+    if r is None:
+        return
+    h, k = r // 4, r % 4
+    cable, diag, rackn = 3 - h, h ^ 2, h ^ 1
+    S = T.sem
+
+    def write(dst_rank, out, in_, sem):
+        d = T.cores[dst_rank]
+        rid, pid = topo.addr(d, core)
+        m = topo.mask(core, d)
+        g.remote_dma(out, in_, sem, S.arrived, pid, rid, m)
+        return bin(m).count("1")
+
+    g.dma_start(T.send[:], T.x[:]).then_inc(S.loaded, 16)
+    g.dma_start(T.land[r], T.x[8 * r:8 * r + 8, :]).then_inc(S.loaded, 16)
+    g.wait_ge(S.loaded, 32)
+
+    total = 0
+    for j in range(4):
+        total += write(4 * cable + k, T.relay[j], T.send[4 * diag + j], S.relayed)
+    for hh in (rackn, cable, h):
+        for j in range(4):
+            d = 4 * hh + j
+            if d != r:
+                total += 2 * write(d, T.land[r], T.send[d], S.arrived)
+    g.wait_ge(S.relayed, 32)
+    for j in range(4):
+        total += 2 * write(4 * rackn + j, T.land[4 * cable + k], T.relay[j], S.arrived)
+    g.wait_ge(S.arrived, total)
+    g.dma_start(T.y[:], T.land[:]).then_inc(S.stored, 16)
+    g.wait_ge(S.stored, 16)

@@ -1,3 +1,5 @@
+from concourse.bass import DstId, RemoteDMATransfer
+
 SCRATCH = {
     "send": ("dram", [16, 128, 4], "float32"),
     "land": ("dram", [16, 128, 4], "float32"),
@@ -14,28 +16,26 @@ def rank_program(g, core, T, topo):
     cable, diag, rackn = 3 - h, h ^ 2, h ^ 1
     S = T.sem
 
-    def write(dst_rank, out, in_, sem):
-        d = T.cores[dst_rank]
-        rid, pid = topo.addr(d, core)
-        m = topo.mask(core, d)
-        g.remote_dma(out, in_, sem, S.arrived, pid, rid, m)
-        return bin(m).count("1")
+    def tr(dst_rank, out, in_, sem, mask):
+        rid, pid = topo.addr(T.cores[dst_rank], core)
+        return RemoteDMATransfer(dst_ids=[DstId(rid=rid, pnc=pid)], dma_engine_mask=mask, remote_sem=sem,
+                                 src=in_, dst=out)
 
     g.dma_start(T.send[:], T.x[:]).then_inc(S.loaded, 16)
     g.dma_start(T.land[r], T.x[8 * r:8 * r + 8, :]).then_inc(S.loaded, 16)
     g.wait_ge(S.loaded, 32)
 
-    total = 0
-    for j in range(4):
-        total += write(4 * cable + k, T.relay[j], T.send[4 * diag + j], S.relayed)
-    for hh in (rackn, cable, h):
-        for j in range(4):
-            d = 4 * hh + j
-            if d != r:
-                total += 2 * write(d, T.land[r], T.send[d], S.arrived)
-    g.wait_ge(S.relayed, 32)
-    for j in range(4):
-        total += 2 * write(4 * rackn + j, T.land[4 * cable + k], T.relay[j], S.arrived)
-    g.wait_ge(S.arrived, total)
+    g.remote_dma_fused([tr(4 * cable + k, T.relay[j], T.send[4 * diag + j], S.relayed, 3 << (2 * j)) for j in range(4)],
+                       local_sem=S.arrived)
+    ts = []
+    for i, d in enumerate([4 * rackn + j for j in range(4)] + [4 * cable + j for j in range(4)]):
+        ts.append(tr(d, T.land[r], T.send[d], S.arrived, 1 << i))
+    for i, d in enumerate([4 * h + j for j in range(4) if j != k]):
+        ts.append(tr(d, T.land[r], T.send[d], S.arrived, 3 << (8 + 2 * i)))
+    g.remote_dma_fused(ts, local_sem=S.arrived)
+    g.wait_ge(S.relayed, 8)
+    g.remote_dma_fused([tr(4 * rackn + j, T.land[4 * cable + k], T.relay[j], S.arrived, 3 << (2 * j)) for j in range(4)],
+                       local_sem=S.arrived)
+    g.wait_ge(S.arrived, 52)
     g.dma_start(T.y[:], T.land[:]).then_inc(S.stored, 16)
     g.wait_ge(S.stored, 16)

@@ -5,7 +5,7 @@ SCRATCH = {
     "land": ("dram", [16, 128, 4], "float32"),
     "relay": ("dram", [4, 128, 4], "float32"),
 }
-SEMAPHORES = ["loaded", "relayed", "arrived", "stored"]
+SEMAPHORES = ["loaded", "own", "relayed", "arrived", "stored"]
 
 
 def rank_program(g, core, T, topo):
@@ -22,8 +22,7 @@ def rank_program(g, core, T, topo):
                                  src=in_, dst=out)
 
     g.dma_start(T.send[:], T.x[:]).then_inc(S.loaded, 16)
-    g.dma_start(T.land[r], T.x[8 * r:8 * r + 8, :]).then_inc(S.loaded, 16)
-    g.wait_ge(S.loaded, 32)
+    g.wait_ge(S.loaded, 16)
 
     g.remote_dma_fused([tr(4 * cable + k, T.relay[j], T.send[4 * diag + j], S.relayed, 3 << (2 * j)) for j in range(4)],
                        local_sem=S.arrived)
@@ -33,9 +32,11 @@ def rank_program(g, core, T, topo):
     for i, d in enumerate([4 * h + j for j in range(4) if j != k]):
         ts.append(tr(d, T.land[r], T.send[d], S.arrived, 3 << (8 + 2 * i)))
     g.remote_dma_fused(ts, local_sem=S.arrived)
+    g.dma_start(T.land[r], T.x[8 * r:8 * r + 8, :]).then_inc(S.own, 16)
     g.wait_ge(S.relayed, 8)
     g.remote_dma_fused([tr(4 * rackn + j, T.land[4 * cable + k], T.relay[j], S.arrived, 3 << (2 * j)) for j in range(4)],
                        local_sem=S.arrived)
+    g.wait_ge(S.own, 16)
     g.wait_ge(S.arrived, 52)
     g.dma_start(T.y[:], T.land[:]).then_inc(S.stored, 16)
     g.wait_ge(S.stored, 16)

@@ -3,9 +3,9 @@ from concourse.bass import DstId, RemoteDMATransfer
 SCRATCH = {
     "send": ("dram", [16, 128, 4], "float32"),
     "land": ("dram", [16, 128, 4], "float32"),
-    "relay": ("dram", [4, 128, 4], "float32"),
+    "relay": ("dram", [5, 128, 4], "float32"),
 }
-SEMAPHORES = ["loaded", "own", "relayed", "arrived", "stored"]
+SEMAPHORES = ["loaded", "relayed", "arrived", "stored"]
 
 
 def rank_program(g, core, T, topo):
@@ -24,19 +24,17 @@ def rank_program(g, core, T, topo):
     g.dma_start(T.send[:], T.x[:]).then_inc(S.loaded, 16)
     g.wait_ge(S.loaded, 16)
 
-    g.remote_dma_fused([tr(4 * cable + k, T.relay[j], T.send[4 * diag + j], S.relayed, 3 << (2 * j)) for j in range(4)],
-                       local_sem=S.arrived)
+    g.remote_dma_fused([tr(4 * cable + k, T.relay[j], T.send[4 * diag + j], S.relayed, 3 << (2 * j)) for j in range(4)]
+                       + [tr(r ^ 1, T.relay[4], T.send[r], S.relayed, 3 << 8)], local_sem=S.arrived)
     ts = []
     for i, d in enumerate([4 * rackn + j for j in range(4)] + [4 * cable + j for j in range(4)]):
         ts.append(tr(d, T.land[r], T.send[d], S.arrived, 1 << i))
     for i, d in enumerate([4 * h + j for j in range(4) if j != k]):
         ts.append(tr(d, T.land[r], T.send[d], S.arrived, 3 << (8 + 2 * i)))
     g.remote_dma_fused(ts, local_sem=S.arrived)
-    g.dma_start(T.land[r], T.x[8 * r:8 * r + 8, :]).then_inc(S.own, 16)
-    g.wait_ge(S.relayed, 8)
-    g.remote_dma_fused([tr(4 * rackn + j, T.land[4 * cable + k], T.relay[j], S.arrived, 3 << (2 * j)) for j in range(4)],
-                       local_sem=S.arrived)
-    g.wait_ge(S.own, 16)
-    g.wait_ge(S.arrived, 52)
+    g.wait_ge(S.relayed, 10)
+    g.remote_dma_fused([tr(4 * rackn + j, T.land[4 * cable + k], T.relay[j], S.arrived, 3 << (2 * j)) for j in range(4)]
+                       + [tr(r ^ 1, T.land[r ^ 1], T.relay[4], S.arrived, 3 << 8)], local_sem=S.arrived)
+    g.wait_ge(S.arrived, 58)
     g.dma_start(T.y[:], T.land[:]).then_inc(S.stored, 16)
     g.wait_ge(S.stored, 16)

@@ -9,32 +9,40 @@ SEMAPHORES = ["loaded", "relayed", "arrived", "stored"]
 
 
 def rank_program(g, core, T, topo):
-    r = T.rank_of(core)
-    if r is None:
-        return
-    h, k = r // 4, r % 4
-    cable, diag, rackn = 3 - h, h ^ 2, h ^ 1
     S = T.sem
+    h, k = topo.host(core), core % 8
+    cable, diag, rackn = 3 - h, h ^ 2, h ^ 1
 
-    def tr(dst_rank, out, in_, sem, mask):
-        rid, pid = topo.addr(T.cores[dst_rank], core)
+    def tr(d, out, in_, sem, mask):
+        rid, pid = topo.addr(d, core)
         return RemoteDMATransfer(dst_ids=[DstId(rid=rid, pnc=pid)], dma_engine_mask=mask, remote_sem=sem,
                                  src=in_, dst=out)
+
+    r = T.rank_of(core)
+    if r is None:
+        if topo.chip(core) == 3 and k < 4:
+            g.wait_ge(S.relayed, 4)
+            g.remote_dma_fused([tr(T.cores[4 * cable + j], T.land[4 * rackn + k], T.relay[j], S.arrived, 15 << (4 * j - 8))
+                                for j in (2, 3)], local_sem=S.relayed)
+            g.wait_ge(S.relayed, 12)
+        return
+    k -= 4
 
     g.dma_start(T.send[:], T.x[:]).then_inc(S.loaded, 16)
     g.wait_ge(S.loaded, 16)
 
-    g.remote_dma_fused([tr(4 * cable + k, T.relay[j], T.send[4 * diag + j], S.relayed, 3 << (2 * j)) for j in range(4)]
-                       + [tr(r ^ 1, T.relay[4], T.send[r], S.relayed, 3 << 8)], local_sem=S.arrived)
+    g.remote_dma_fused([tr(T.cores[4 * cable + k], T.relay[j], T.send[4 * diag + j], S.relayed, 3 << (2 * j)) for j in (0, 1)]
+                       + [tr(128 * rackn + 24 + k, T.relay[j], T.send[4 * diag + j], S.relayed, 3 << (2 * j)) for j in (2, 3)]
+                       + [tr(T.cores[r ^ 1], T.relay[4], T.send[r], S.relayed, 3 << 8)], local_sem=S.arrived)
     ts = []
     for i, d in enumerate([4 * rackn + j for j in range(4)] + [4 * cable + j for j in range(4)]):
-        ts.append(tr(d, T.land[r], T.send[d], S.arrived, 1 << i))
+        ts.append(tr(T.cores[d], T.land[r], T.send[d], S.arrived, 1 << i))
     for i, d in enumerate([4 * h + j for j in range(4) if j != k]):
-        ts.append(tr(d, T.land[r], T.send[d], S.arrived, 3 << (8 + 2 * i)))
+        ts.append(tr(T.cores[d], T.land[r], T.send[d], S.arrived, 3 << (8 + 2 * i)))
     g.remote_dma_fused(ts, local_sem=S.arrived)
-    g.wait_ge(S.relayed, 10)
-    g.remote_dma_fused([tr(4 * rackn + j, T.land[4 * cable + k], T.relay[j], S.arrived, 3 << (2 * j)) for j in range(4)]
-                       + [tr(r ^ 1, T.land[r ^ 1], T.relay[4], S.arrived, 3 << 8)], local_sem=S.arrived)
-    g.wait_ge(S.arrived, 58)
+    g.wait_ge(S.relayed, 6)
+    g.remote_dma_fused([tr(T.cores[4 * rackn + j], T.land[4 * cable + k], T.relay[j], S.arrived, 15 << (4 * j)) for j in (0, 1)]
+                       + [tr(T.cores[r ^ 1], T.land[r ^ 1], T.relay[4], S.arrived, 3 << 8)], local_sem=S.arrived)
+    g.wait_ge(S.arrived, 66)
     g.dma_start(T.y[:], T.land[:]).then_inc(S.stored, 16)
     g.wait_ge(S.stored, 16)

from concourse.bass import DstId, RemoteDMATransfer

SCRATCH = {
    "send": ("dram", [16, 128, 4], "float32"),
    "land": ("dram", [16, 128, 4], "float32"),
    "relay": ("dram", [5, 128, 4], "float32"),
}
SEMAPHORES = ["loaded", "relayed", "arrived", "stored"]


def rank_program(g, core, T, topo):
    S = T.sem
    h, k = topo.host(core), core % 8
    cable, diag, rackn = 3 - h, h ^ 2, h ^ 1

    def tr(d, out, in_, sem, mask):
        rid, pid = topo.addr(d, core)
        return RemoteDMATransfer(dst_ids=[DstId(rid=rid, pnc=pid)], dma_engine_mask=mask, remote_sem=sem,
                                 src=in_, dst=out)

    r = T.rank_of(core)
    if r is None:
        if topo.chip(core) == 3 and k < 4:
            g.wait_ge(S.relayed, 4)
            g.remote_dma_fused([tr(T.cores[4 * cable + j], T.land[4 * rackn + k], T.relay[j], S.arrived, 15 << (4 * j - 8))
                                for j in (2, 3)], local_sem=S.relayed)
            g.wait_ge(S.relayed, 12)
        return
    k -= 4

    g.dma_start(T.send[:], T.x[:]).then_inc(S.loaded, 16)
    g.wait_ge(S.loaded, 16)

    g.remote_dma_fused([tr(T.cores[4 * cable + k], T.relay[j], T.send[4 * diag + j], S.relayed, 3 << (2 * j)) for j in (0, 1)]
                       + [tr(128 * rackn + 24 + k, T.relay[j], T.send[4 * diag + j], S.relayed, 3 << (2 * j)) for j in (2, 3)]
                       + [tr(T.cores[r ^ 1], T.relay[4], T.send[r], S.relayed, 3 << 8)], local_sem=S.arrived)
    ts = []
    for i, d in enumerate([4 * rackn + j for j in range(4)] + [4 * cable + j for j in range(4)]):
        ts.append(tr(T.cores[d], T.land[r], T.send[d], S.arrived, 1 << i))
    for i, d in enumerate([4 * h + j for j in range(4) if j != k]):
        ts.append(tr(T.cores[d], T.land[r], T.send[d], S.arrived, 3 << (8 + 2 * i)))
    g.remote_dma_fused(ts, local_sem=S.arrived)
    g.wait_ge(S.relayed, 6)
    g.remote_dma_fused([tr(T.cores[4 * rackn + j], T.land[4 * cable + k], T.relay[j], S.arrived, 15 << (4 * j)) for j in (0, 1)]
                       + [tr(T.cores[r ^ 1], T.land[r ^ 1], T.relay[4], S.arrived, 3 << 8)], local_sem=S.arrived)
    g.wait_ge(S.arrived, 66)
    g.dma_start(T.y[:], T.land[:]).then_inc(S.stored, 16)
    g.wait_ge(S.stored, 16)
